import numpy as np
CORES = [2,10,50,58,66,74,122]
N = 7
TK = 128
D = 128 * N
EPS = 0.01
def setup_inputs(rng):
    return {"x": (rng.standard_normal((N, 128, TK), dtype=np.float32) * (0.5 + np.abs(rng.standard_normal((1, 1, TK), dtype=np.float32))) + rng.standard_normal((1, 1, TK), dtype=np.float32)), "w": (rng.standard_normal((N, 128, 128), dtype=np.float32) / 11)}
def setup_inputs_big(rng):
    d = setup_inputs(rng)
    for k in ("x", "w"): d[k] = (d[k].astype(np.float32) * 1024.0).astype(d[k].dtype)
    return d
def setup_inputs_small(rng):
    d = setup_inputs(rng)
    for k in ("x", "w"): d[k] = (d[k].astype(np.float32) * (1 / 1024.0)).astype(d[k].dtype)
    return d
def setup_inputs_apart(rng):
    d = setup_inputs(rng)
    f = (10.0 ** rng.permutation(np.linspace(-1.5, 1.5, N))).astype(np.float32).reshape(N, 1, 1)
    for k in ("x", "w"): d[k] = (d[k].astype(np.float32) * f).astype(d[k].dtype)
    return d
def setup_inputs_mixed(rng):
    d = setup_inputs(rng)
    f = (10.0 ** rng.uniform(-3, 3, (1, 1, TK))).astype(np.float32); shape = rng.integers(3, size=(1, 1, TK))
    for k in ("x",):
        x = d[k].astype(np.float32)
        m = x.mean(axis=(0, 1), keepdims=True); level = m + np.sign(x - m) * np.abs(x - m).mean(axis=(0, 1), keepdims=True) * rng.uniform(0.9, 1.1, x.shape).astype(np.float32)
        other = x * np.where(rng.random(x.shape) < 0.5, 0.1, 1.0).astype(np.float32)
        d[k] = (np.where(shape == 1, level, np.where(shape == 2, other, x)) * f).astype(d[k].dtype)
    return d
def setup_inputs_offset(rng):
    d = setup_inputs(rng)
    x = d["x"]; spread = x.std(axis=(0, 1), keepdims=True)
    d["x"] = (x + spread * rng.uniform(16, 48, (1, 1, TK)) * rng.choice([-1.0, 1.0], (1, 1, TK))).astype(np.float32)
    return d
def reference(x, w):
    X = x.astype(np.float64)
    mu = X.sum(axis=(0, 1)) / D
    Z = X - mu
    Z = Z / np.sqrt((Z ** 2).sum(axis=(0, 1)) / D + EPS)
    s = sum(w[r].astype(np.float64).T @ Z[r] for r in range(N)).astype(np.float32)
    return {"y": np.broadcast_to(s, (N,) + s.shape)}

@@ -1,0 +1,168 @@
+from concourse.bass import DstId, RemoteDMATransfer
+from concourse.mybir import AluOpType, AxisListType, ActivationFunctionType
+
+N = 7
+W = 132
+WS = 131
+D = 128 * N
+EPS = 0.01
+
+SCRATCH = {
+    "xs": ("sbuf", [128, 128], "float32"),
+    "ws": ("sbuf", [128, 128], "float32"),
+    "o128": ("sbuf", [128, 128], "float32"),
+    "onesT": ("sbuf", [128, 128], "float32"),
+    "ident": ("sbuf", [128, 128], "float32"),
+    "cst": ("sbuf", [128, 4], "float32"),
+    "z": ("sbuf", [128, 128], "float32"),
+    "z2": ("sbuf", [128, 128], "float32"),
+    "tmpd": ("sbuf", [128, 128], "float32"),
+    "land": ("sbuf", [128, N * W], "float32"),
+    "negmus": ("sbuf", [128, 4], "float32"),
+    "q": ("sbuf", [128, 4], "float32"),
+    "qp": ("sbuf", [128, 4], "float32"),
+    "d7": ("sbuf", [128, 8], "float32"),
+    "junk7": ("sbuf", [128, 8], "float32"),
+    "sd49": ("sbuf", [128, 4], "float32"),
+    "v": ("sbuf", [128, 4], "float32"),
+    "rv": ("sbuf", [128, 4], "float32"),
+    "diag": ("sbuf", [128, 128], "float32"),
+    "tr": ("sbuf", [128, 256], "float32"),
+    "s0": ("sbuf", [128, 128], "float32"),
+    "s1": ("sbuf", [128, 128], "float32"),
+    "ysb": ("sbuf", [128, 128], "float32"),
+    "p_mb": ("psum", [128, 512], "float32"),
+    "p_pt": ("psum", [128, 512], "float32"),
+    "p_st": ("psum", [128, 512], "float32"),
+    "p_tr": ("psum", [128, 512], "float32"),
+    "p_corr": ("psum", [128, 512], "float32"),
+    "p_y": ("psum", [128, 512], "float32"),
+}
+SEMAPHORES = ["x", "w", "c1", "c2", "c3", "id", "mb", "cw", "z", "pt", "z2", "m2", "td", "cc", "cp1", "cp2",
+              "sent", "arr", "v1", "v0", "v2", "qp", "sq", "v3", "v4", "diag", "add", "tr", "trc", "corr",
+              "sum", "y", "yc", "st"]
+
+
+def rank_program(g, core, T, topo):
+    rank = T.rank_of(core)
+    if rank is None:
+        return
+    s = T.sem
+    V, PE, ACT, SY = g.vector, g.tensor, g.scalar, g.sync
+    add, mult = AluOpType.add, AluOpType.mult
+    AF = ActivationFunctionType
+    o = rank * W
+    own = T.land[:, o:o + WS]
+    Mc = T.land[:, 128::W]
+    Qc = T.land[:, 129::W]
+    Wc = T.land[:, 130::W]
+    others = [T.cores[(rank + k) % N] for k in range(1, N)]
+    mask = topo.mask(core, others[0])
+    for c in others:
+        if not topo.may_write(core, c):
+            raise ValueError("rank core cannot reach a rank")
+        mask &= topo.mask(core, c)
+    n_eng = bin(mask).count("1")
+
+    SY.dma_start(T.xs[:], T.x[:]).then_inc(s.x, 16)
+    ACT.dma_start(T.ws[:], T.w[:]).then_inc(s.w, 16)
+    V.memset(T.o128[:], 1.0 / 128).then_inc(s.c1, 1)
+    V.memset(T.onesT[:], 1.0).then_inc(s.c3, 1)
+    V.memset(T.cst[:, 0:1], 1.0).then_inc(s.c2, 1)
+    V.memset(T.cst[:, 1:2], 1.0 / N).then_inc(s.c2, 1)
+    g.wait_ge(s.c3, 1)
+    g.affine_select(T.ident[:], T.onesT[:], [[-1, 128]], AluOpType.is_equal, 0.0, 0, 1).then_inc(s.id, 1)
+
+    PE.wait_ge(s.x, 16)
+    PE.wait_ge(s.c1, 1)
+    PE.matmul(T.p_mb[:, 0:128], T.o128[:], T.xs[:], True, True).then_inc(s.mb, 1)
+    PE.wait_ge(s.w, 16)
+    PE.wait_ge(s.c2, 2)
+    PE.matmul(T.p_st[:, 1:2], T.ws[:], T.cst[:, 1:2], True, True).then_inc(s.cw, 1)
+    V.wait_ge(s.x, 16)
+    V.wait_ge(s.mb, 1)
+    V.tensor_tensor(T.z[:], T.xs[:], T.p_mb[:, 0:128], AluOpType.subtract).then_inc(s.z, 1)
+    PE.wait_ge(s.z, 1)
+    PE.matmul(T.p_pt[:, 0:128], T.z[:], T.ws[:], True, True).then_inc(s.pt, 1)
+    ACT.wait_ge(s.z, 1)
+    ACT.activation(T.z2[:], T.z[:], AF.Square).then_inc(s.z2, 1)
+    PE.wait_ge(s.z2, 1)
+    PE.matmul(T.p_st[:, 0:1], T.z2[:], T.cst[:, 0:1], True, True).then_inc(s.m2, 1)
+    V.wait_ge(s.id, 1)
+    V.tensor_tensor(T.tmpd[:], T.ident[:], T.p_mb[:, 0:128], mult).then_inc(s.td, 1)
+    V.wait_ge(s.td, 1)
+    V.tensor_reduce(T.land[:, o + 128:o + 129], T.tmpd[:], AxisListType.X, add).then_inc(s.cc, 1)
+    V.wait_ge(s.pt, 1)
+    V.tensor_copy(T.land[:, o:o + 128], T.p_pt[:, 0:128]).then_inc(s.cp1, 1)
+    V.wait_ge(s.m2, 1)
+    V.wait_ge(s.cw, 1)
+    V.tensor_copy(T.land[:, o + 129:o + 131], T.p_st[:, 0:2]).then_inc(s.cp2, 1)
+
+    g.wait_ge(s.cc, 1)
+    g.wait_ge(s.cp1, 1)
+    g.wait_ge(s.cp2, 1)
+    ids = []
+    for c in others:
+        rid, pid, _se = topo.addr(c)
+        ids.append(DstId(rid=rid, pnc=pid))
+    g.remote_dma_fused([RemoteDMATransfer(dst_ids=ids, dma_engine_mask=mask, remote_sem=s.arr,
+                                          srcs=[own], dsts=[own for _c in others], alu_op=0)], local_sem=s.sent)
+    g.wait_ge(s.sent, n_eng)
+    all_in = n_eng * (N - 1)
+
+    V.wait_ge(s.cc, 1)
+    V.wait_ge(s.cp1, 1)
+    V.wait_ge(s.cp2, 1)
+    V.wait_ge(s.arr, all_in)
+    V.tensor_reduce(T.negmus[:, 0:1], Mc, AxisListType.X, add, negate=True).then_inc(s.v1, 1)
+    V.tensor_reduce(T.q[:, 0:1], Qc, AxisListType.X, add).then_inc(s.v0, 1)
+    V.wait_ge(s.v1, 1)
+    V.tensor_scalar(T.d7[:, 0:N], Mc, float(N), T.negmus[:, 0:1], mult, add).then_inc(s.v2, 1)
+    V.wait_ge(s.v0, 1)
+    V.tensor_scalar(T.qp[:, 0:1], T.q[:, 0:1], 1.0 / D, EPS, mult, add).then_inc(s.qp, 1)
+    ACT.wait_ge(s.cc, 1)
+    ACT.wait_ge(s.arr, all_in)
+    ACT.wait_ge(s.v1, 1)
+    ACT.activation(T.junk7[:, 0:N], Mc, AF.Square, bias=T.negmus[:, 0:1], scale=float(N),
+                   accum_out=T.sd49[:, 0:1]).then_inc(s.sq, 1)
+    V.wait_ge(s.sq, 1)
+    V.wait_ge(s.qp, 1)
+    V.tensor_scalar(T.v[:, 0:1], T.sd49[:, 0:1], 128.0 / (N * N * D), T.qp[:, 0:1], mult, add).then_inc(s.v3, 1)
+    V.wait_ge(s.v3, 1)
+    V.reciprocal(T.rv[:, 0:1], T.v[:, 0:1]).then_inc(s.v4, 1)
+    ACT.wait_ge(s.v4, 1)
+    ACT.wait_ge(s.id, 1)
+    ACT.activation(T.diag[:], T.ident[:], AF.Sqrt, scale=T.rv[:, 0:1]).then_inc(s.diag, 1)
+
+    PE.wait_ge(s.cp2, 1)
+    PE.wait_ge(s.arr, all_in)
+    PE.wait_ge(s.id, 1)
+    PE.matmul(T.p_tr[0:N, 128:256], Wc, T.ident[:], True, True).then_inc(s.tr, 1)
+    PE.wait_ge(s.v2, 1)
+    PE.matmul(T.p_tr[0:N, 0:128], T.d7[:, 0:N], T.ident[:], True, True).then_inc(s.tr, 1)
+
+    order = [(rank - k) % N for k in range(1, N)]
+    n_add = 0
+    for i, j in enumerate(order):
+        if i == 3:
+            V.wait_ge(s.tr, 2)
+            V.tensor_copy(T.tr[0:N, 0:256], T.p_tr[0:N, 0:256]).then_inc(s.trc, 1)
+        if n_add:
+            V.wait_ge(s.add, n_add)
+        out = T.s0[:] if i == N - 2 else T.p_pt[:, 0:128]
+        V.tensor_tensor(out, T.land[:, j * W:j * W + 128], T.p_pt[:, 0:128], add).then_inc(s.add, 1)
+        n_add += 1
+    PE.wait_ge(s.trc, 1)
+    PE.matmul(T.p_corr[:, 0:128], T.tr[0:N, 0:128], T.tr[0:N, 128:256], True, True).then_inc(s.corr, 1)
+    V.wait_ge(s.add, n_add)
+    V.wait_ge(s.corr, 1)
+    V.tensor_tensor(T.s1[:], T.s0[:], T.p_corr[:, 0:128], add).then_inc(s.sum, 1)
+
+    PE.wait_ge(s.sum, 1)
+    PE.wait_ge(s.diag, 1)
+    PE.matmul(T.p_y[:, 0:128], T.s1[:], T.diag[:], True, True).then_inc(s.y, 1)
+    V.wait_ge(s.y, 1)
+    V.tensor_copy(T.ysb[:], T.p_y[:, 0:128]).then_inc(s.yc, 1)
+    SY.wait_ge(s.yc, 1)
+    SY.dma_start(T.y[:], T.ysb[:]).then_inc(s.st, 16)
+    SY.wait_ge(s.st, 16)

@@ -2,8 +2,12 @@ from concourse.bass import DstId, RemoteDMATransfer
 from concourse.mybir import AluOpType, AxisListType, ActivationFunctionType
 
 N = 7
-W = 132
-WS = 131
+PW = 20
+WIN = 24
+NP = N * PW
+NZ = NP + 4
+PER = 2 * PW + 4
+SNDW = PER * (N // 2) + WIN
 D = 128 * N
 EPS = 0.01
 
@@ -13,22 +17,29 @@ SCRATCH = {
     "o128": ("sbuf", [128, 128], "float32"),
     "onesT": ("sbuf", [128, 128], "float32"),
     "ident": ("sbuf", [128, 128], "float32"),
-    "cst": ("sbuf", [128, 4], "float32"),
-    "z": ("sbuf", [128, 128], "float32"),
+    "cst": ("sbuf", [128, 8], "float32"),
+    "z": ("sbuf", [128, NZ], "float32"),
     "z2": ("sbuf", [128, 128], "float32"),
     "tmpd": ("sbuf", [128, 128], "float32"),
-    "land": ("sbuf", [128, N * W], "float32"),
-    "negmus": ("sbuf", [128, 4], "float32"),
-    "q": ("sbuf", [128, 4], "float32"),
+    "ccol": ("sbuf", [128, 4], "float32"),
+    "snd": ("sbuf", [128, SNDW], "float32"),
+    "land1": ("sbuf", [128, N * WIN], "float32"),
+    "t1": ("sbuf", [128, 3 * WIN], "float32"),
+    "t2": ("sbuf", [128, WIN], "float32"),
+    "t3": ("sbuf", [128, WIN], "float32"),
+    "tot": ("sbuf", [128, WIN], "float32"),
+    "sg": ("sbuf", [128, NP], "float32"),
+    "mus": ("sbuf", [128, 4], "float32"),
     "qp": ("sbuf", [128, 4], "float32"),
     "d7": ("sbuf", [128, 8], "float32"),
+    "junka": ("sbuf", [128, 8], "float32"),
+    "junkb": ("sbuf", [128, 8], "float32"),
     "junk7": ("sbuf", [128, 8], "float32"),
     "sd49": ("sbuf", [128, 4], "float32"),
-    "v": ("sbuf", [128, 4], "float32"),
-    "rv": ("sbuf", [128, 4], "float32"),
+    "sroot": ("sbuf", [128, 4], "float32"),
+    "rstd": ("sbuf", [128, 4], "float32"),
     "diag": ("sbuf", [128, 128], "float32"),
     "tr": ("sbuf", [128, 256], "float32"),
-    "s0": ("sbuf", [128, 128], "float32"),
     "s1": ("sbuf", [128, 128], "float32"),
     "ysb": ("sbuf", [128, 128], "float32"),
     "p_mb": ("psum", [128, 512], "float32"),
@@ -36,11 +47,15 @@ SCRATCH = {
     "p_st": ("psum", [128, 512], "float32"),
     "p_tr": ("psum", [128, 512], "float32"),
     "p_corr": ("psum", [128, 512], "float32"),
-    "p_y": ("psum", [128, 512], "float32"),
+    "p_r": ("psum", [128, 512], "float32"),
 }
-SEMAPHORES = ["x", "w", "c1", "c2", "c3", "id", "mb", "cw", "z", "pt", "z2", "m2", "td", "cc", "cp1", "cp2",
-              "sent", "arr", "v1", "v0", "v2", "qp", "sq", "v3", "v4", "diag", "add", "tr", "trc", "corr",
-              "sum", "y", "yc", "st"]
+SEMAPHORES = ["x", "w", "c1", "c2", "c3", "c4", "c5", "id", "mb", "z", "pt", "z2", "m2", "td", "cc", "st3", "cp1",
+              "ownw", "sent1", "sent2", "arr1", "arr2", "t1", "t23", "tot", "ownp", "v2", "a1", "a3", "sq", "s2", "v4",
+              "diag", "tr", "trc", "corr", "sum", "r", "yc", "st"]
+
+
+def win_start(j):
+    return PER * (j // 2) + (0 if j % 2 == 0 else PW)
 
 
 def rank_program(g, core, T, topo):
@@ -49,120 +64,149 @@ def rank_program(g, core, T, topo):
         return
     s = T.sem
     V, PE, ACT, SY = g.vector, g.tensor, g.scalar, g.sync
-    add, mult = AluOpType.add, AluOpType.mult
+    add, mult, sub = AluOpType.add, AluOpType.mult, AluOpType.subtract
     AF = ActivationFunctionType
-    o = rank * W
-    own = T.land[:, o:o + WS]
-    Mc = T.land[:, 128::W]
-    Qc = T.land[:, 129::W]
-    Wc = T.land[:, 130::W]
-    others = [T.cores[(rank + k) % N] for k in range(1, N)]
-    mask = topo.mask(core, others[0])
-    for c in others:
-        if not topo.may_write(core, c):
+    po = 0 if rank % 2 == 0 else 4
+    so = PW if rank % 2 == 0 else 0
+    Mc = T.land1[:, so::WIN]
+    Qc = T.land1[:, so + 1::WIN]
+    Wc = T.land1[:, so + 2::WIN]
+    others = [(rank + k) % N for k in range(1, N)]
+    mask = topo.mask(core, T.cores[others[0]])
+    for d in others:
+        if not topo.may_write(core, T.cores[d]):
             raise ValueError("rank core cannot reach a rank")
-        mask &= topo.mask(core, c)
-    n_eng = bin(mask).count("1")
+        mask &= topo.mask(core, T.cores[d])
+    bits = [b for b in range(16) if (mask >> b) & 1]
+    n_eng = len(bits)
+    ids = {}
+    for d in others:
+        rid, pid, _se = topo.addr(T.cores[d])
+        ids[d] = DstId(rid=rid, pnc=pid)
 
     SY.dma_start(T.xs[:], T.x[:]).then_inc(s.x, 16)
     ACT.dma_start(T.ws[:], T.w[:]).then_inc(s.w, 16)
     V.memset(T.o128[:], 1.0 / 128).then_inc(s.c1, 1)
     V.memset(T.onesT[:], 1.0).then_inc(s.c3, 1)
-    V.memset(T.cst[:, 0:1], 1.0).then_inc(s.c2, 1)
-    V.memset(T.cst[:, 1:2], 1.0 / N).then_inc(s.c2, 1)
+    V.memset(T.cst[:, 0:4], 1.0).then_inc(s.c2, 1)
+    V.memset(T.cst[:, 4:8], 1.0 / D).then_inc(s.c2, 1)
+    V.memset(T.z[:, 128:NP], 0.0).then_inc(s.c5, 1)
+    V.memset(T.z[:, NP:NZ], 1.0 / N).then_inc(s.c5, 1)
+    V.memset(T.snd[:], 0.0).then_inc(s.c4, 1)
     g.wait_ge(s.c3, 1)
     g.affine_select(T.ident[:], T.onesT[:], [[-1, 128]], AluOpType.is_equal, 0.0, 0, 1).then_inc(s.id, 1)
 
     PE.wait_ge(s.x, 16)
     PE.wait_ge(s.c1, 1)
     PE.matmul(T.p_mb[:, 0:128], T.o128[:], T.xs[:], True, True).then_inc(s.mb, 1)
-    PE.wait_ge(s.w, 16)
-    PE.wait_ge(s.c2, 2)
-    PE.matmul(T.p_st[:, 1:2], T.ws[:], T.cst[:, 1:2], True, True).then_inc(s.cw, 1)
     V.wait_ge(s.x, 16)
     V.wait_ge(s.mb, 1)
-    V.tensor_tensor(T.z[:], T.xs[:], T.p_mb[:, 0:128], AluOpType.subtract).then_inc(s.z, 1)
+    V.tensor_tensor(T.z[:, 0:128], T.xs[:], T.p_mb[:, 0:128], sub).then_inc(s.z, 1)
+    PE.wait_ge(s.w, 16)
+    PE.wait_ge(s.c5, 2)
     PE.wait_ge(s.z, 1)
-    PE.matmul(T.p_pt[:, 0:128], T.z[:], T.ws[:], True, True).then_inc(s.pt, 1)
+    PE.matmul(T.p_pt[:, 0:NZ], T.ws[:], T.z[:], True, True).then_inc(s.pt, 1)
     ACT.wait_ge(s.z, 1)
-    ACT.activation(T.z2[:], T.z[:], AF.Square).then_inc(s.z2, 1)
+    ACT.activation(T.z2[:], T.z[:, 0:128], AF.Square).then_inc(s.z2, 1)
     PE.wait_ge(s.z2, 1)
-    PE.matmul(T.p_st[:, 0:1], T.z2[:], T.cst[:, 0:1], True, True).then_inc(s.m2, 1)
+    PE.wait_ge(s.c2, 2)
+    PE.matmul(T.p_st[:, 0:4], T.z2[:], T.cst[:, 4:8], True, True).then_inc(s.m2, 1)
     V.wait_ge(s.id, 1)
     V.tensor_tensor(T.tmpd[:], T.ident[:], T.p_mb[:, 0:128], mult).then_inc(s.td, 1)
     V.wait_ge(s.td, 1)
-    V.tensor_reduce(T.land[:, o + 128:o + 129], T.tmpd[:], AxisListType.X, add).then_inc(s.cc, 1)
-    V.wait_ge(s.pt, 1)
-    V.tensor_copy(T.land[:, o:o + 128], T.p_pt[:, 0:128]).then_inc(s.cp1, 1)
-    V.wait_ge(s.m2, 1)
-    V.wait_ge(s.cw, 1)
-    V.tensor_copy(T.land[:, o + 129:o + 131], T.p_st[:, 0:2]).then_inc(s.cp2, 1)
-
-    g.wait_ge(s.cc, 1)
-    g.wait_ge(s.cp1, 1)
-    g.wait_ge(s.cp2, 1)
-    ids = []
-    for c in others:
-        rid, pid, _se = topo.addr(c)
-        ids.append(DstId(rid=rid, pnc=pid))
-    g.remote_dma_fused([RemoteDMATransfer(dst_ids=ids, dma_engine_mask=mask, remote_sem=s.arr,
-                                          srcs=[own], dsts=[own for _c in others], alu_op=0)], local_sem=s.sent)
-    g.wait_ge(s.sent, n_eng)
-    all_in = n_eng * (N - 1)
-
+    V.tensor_reduce(T.ccol[:, 0:1], T.tmpd[:], AxisListType.X, add).then_inc(s.cc, 1)
     V.wait_ge(s.cc, 1)
-    V.wait_ge(s.cp1, 1)
-    V.wait_ge(s.cp2, 1)
-    V.wait_ge(s.arr, all_in)
-    V.tensor_reduce(T.negmus[:, 0:1], Mc, AxisListType.X, add, negate=True).then_inc(s.v1, 1)
-    V.tensor_reduce(T.q[:, 0:1], Qc, AxisListType.X, add).then_inc(s.v0, 1)
-    V.wait_ge(s.v1, 1)
-    V.tensor_scalar(T.d7[:, 0:N], Mc, float(N), T.negmus[:, 0:1], mult, add).then_inc(s.v2, 1)
-    V.wait_ge(s.v0, 1)
-    V.tensor_scalar(T.qp[:, 0:1], T.q[:, 0:1], 1.0 / D, EPS, mult, add).then_inc(s.qp, 1)
-    ACT.wait_ge(s.cc, 1)
-    ACT.wait_ge(s.arr, all_in)
-    ACT.wait_ge(s.v1, 1)
-    ACT.activation(T.junk7[:, 0:N], Mc, AF.Square, bias=T.negmus[:, 0:1], scale=float(N),
+    V.wait_ge(s.c2, 2)
+    V.wait_ge(s.c4, 1)
+    V.tensor_scalar(T.snd[:, PW::PER], T.cst[:, 0:4], T.ccol[:, 0:1], None, mult).then_inc(s.st3, 1)
+    V.wait_ge(s.pt, 1)
+    runs = [(0, PW)] + [(PW + 2 * PW * i, 3 * PW + 2 * PW * i) for i in range(N // 2)]
+    for a, b in runs:
+        ja = a // PW
+        pa = PER * (ja // 2) + (0 if ja % 2 == 0 else WIN)
+        V.tensor_copy(T.snd[:, pa:pa + (b - a)], T.p_pt[:, a:b]).then_inc(s.cp1, 1)
+    V.tensor_copy(T.snd[:, PW + 2::PER], T.p_pt[:, NP:NZ]).then_inc(s.st3, 1)
+    ACT.wait_ge(s.c4, 1)
+    ACT.wait_ge(s.m2, 1)
+    ACT.activation(T.snd[:, PW + 1::PER], T.p_st[:, 0:4], AF.Identity, bias=EPS / N).then_inc(s.st3, 1)
+
+    g.wait_ge(s.st3, 3)
+    g.wait_ge(s.cp1, len(runs))
+    slot = T.land1[:, rank * WIN:(rank + 1) * WIN]
+
+    def window_to(d, engines):
+        m = 0
+        for b in engines:
+            m |= 1 << b
+        return RemoteDMATransfer(dst_ids=[ids[d]], dma_engine_mask=m, remote_sem=s.arr1,
+                                 srcs=[T.snd[:, win_start(d):win_start(d) + WIN]], dsts=[slot], alu_op=0)
+
+    q4, h2 = n_eng // 4, n_eng // 2
+    g.remote_dma_fused([window_to(others[i], bits[i * q4:(i + 1) * q4]) for i in range(4)], local_sem=s.sent1)
+    g.remote_dma_fused([window_to(others[4 + i], bits[i * h2:(i + 1) * h2]) for i in range(2)], local_sem=s.sent1)
+    in1 = 4 * q4 + 2 * h2
+    V.wait_ge(s.st3, 3)
+    V.wait_ge(s.cp1, len(runs))
+    V.tensor_copy(slot, T.snd[:, win_start(rank):win_start(rank) + WIN]).then_inc(s.ownw, 1)
+
+    V.wait_ge(s.ownw, 1)
+    V.wait_ge(s.arr1, in1)
+    V.tensor_tensor(T.t1[:], T.land1[:, 0:3 * WIN], T.land1[:, 3 * WIN:6 * WIN], add).then_inc(s.t1, 1)
+    V.wait_ge(s.t1, 1)
+    V.tensor_tensor(T.t2[:], T.t1[:, 0:WIN], T.t1[:, WIN:2 * WIN], add).then_inc(s.t23, 1)
+    V.tensor_tensor(T.t3[:], T.t1[:, 2 * WIN:3 * WIN], T.land1[:, 6 * WIN:7 * WIN], add).then_inc(s.t23, 1)
+    V.wait_ge(s.t23, 2)
+    V.tensor_tensor(T.tot[:], T.t2[:], T.t3[:], add).then_inc(s.tot, 1)
+
+    g.wait_ge(s.tot, 1)
+    piece = T.sg[:, rank * PW:(rank + 1) * PW]
+    g.remote_dma_fused([RemoteDMATransfer(dst_ids=[ids[d] for d in others], dma_engine_mask=mask, remote_sem=s.arr2,
+                                          srcs=[T.tot[:, po:po + PW]], dsts=[piece for _d in others], alu_op=0)],
+                       local_sem=s.sent2)
+    g.wait_ge(s.sent1, in1)
+    g.wait_ge(s.sent2, n_eng)
+
+    ACT.wait_ge(s.ownw, 1)
+    ACT.wait_ge(s.arr1, in1)
+    ACT.activation(T.junka[:, 0:N], Mc, AF.Identity, accum_out=T.mus[:, 0:1]).then_inc(s.a1, 1)
+    ACT.activation(T.junkb[:, 0:N], Qc, AF.Identity, accum_out=T.qp[:, 0:1]).then_inc(s.a3, 1)
+    ACT.wait_ge(s.a1, 1)
+    ACT.activation(T.junk7[:, 0:N], Mc, AF.Square, bias=T.mus[:, 0:1], scale=-float(N),
                    accum_out=T.sd49[:, 0:1]).then_inc(s.sq, 1)
-    V.wait_ge(s.sq, 1)
-    V.wait_ge(s.qp, 1)
-    V.tensor_scalar(T.v[:, 0:1], T.sd49[:, 0:1], 128.0 / (N * N * D), T.qp[:, 0:1], mult, add).then_inc(s.v3, 1)
-    V.wait_ge(s.v3, 1)
-    V.reciprocal(T.rv[:, 0:1], T.v[:, 0:1]).then_inc(s.v4, 1)
+    ACT.wait_ge(s.sq, 1)
+    ACT.wait_ge(s.a3, 1)
+    ACT.activation(T.sroot[:, 0:1], T.sd49[:, 0:1], AF.Sqrt, bias=T.qp[:, 0:1],
+                   scale=128.0 / (N * N * D)).then_inc(s.s2, 1)
     ACT.wait_ge(s.v4, 1)
     ACT.wait_ge(s.id, 1)
-    ACT.activation(T.diag[:], T.ident[:], AF.Sqrt, scale=T.rv[:, 0:1]).then_inc(s.diag, 1)
+    ACT.activation(T.diag[:], T.ident[:], AF.Identity, scale=T.rstd[:, 0:1]).then_inc(s.diag, 1)
 
-    PE.wait_ge(s.cp2, 1)
-    PE.wait_ge(s.arr, all_in)
+    V.wait_ge(s.tot, 1)
+    V.tensor_scalar(T.d7[:, 0:N], Mc, float(N), T.tot[:, so:so + 1], mult, sub).then_inc(s.v2, 1)
+    V.tensor_copy(piece, T.tot[:, po:po + PW]).then_inc(s.ownp, 1)
+    PE.wait_ge(s.ownw, 1)
+    PE.wait_ge(s.arr1, in1)
     PE.wait_ge(s.id, 1)
     PE.matmul(T.p_tr[0:N, 128:256], Wc, T.ident[:], True, True).then_inc(s.tr, 1)
     PE.wait_ge(s.v2, 1)
     PE.matmul(T.p_tr[0:N, 0:128], T.d7[:, 0:N], T.ident[:], True, True).then_inc(s.tr, 1)
-
-    order = [(rank - k) % N for k in range(1, N)]
-    n_add = 0
-    for i, j in enumerate(order):
-        if i == 3:
-            V.wait_ge(s.tr, 2)
-            V.tensor_copy(T.tr[0:N, 0:256], T.p_tr[0:N, 0:256]).then_inc(s.trc, 1)
-        if n_add:
-            V.wait_ge(s.add, n_add)
-        out = T.s0[:] if i == N - 2 else T.p_pt[:, 0:128]
-        V.tensor_tensor(out, T.land[:, j * W:j * W + 128], T.p_pt[:, 0:128], add).then_inc(s.add, 1)
-        n_add += 1
+    V.wait_ge(s.tr, 2)
+    V.tensor_copy(T.tr[0:N, 0:256], T.p_tr[0:N, 0:256]).then_inc(s.trc, 1)
     PE.wait_ge(s.trc, 1)
-    PE.matmul(T.p_corr[:, 0:128], T.tr[0:N, 0:128], T.tr[0:N, 128:256], True, True).then_inc(s.corr, 1)
-    V.wait_ge(s.add, n_add)
-    V.wait_ge(s.corr, 1)
-    V.tensor_tensor(T.s1[:], T.s0[:], T.p_corr[:, 0:128], add).then_inc(s.sum, 1)
-
-    PE.wait_ge(s.sum, 1)
+    PE.matmul(T.p_corr[:, 0:128], T.tr[0:N, 128:256], T.tr[0:N, 0:128], True, True).then_inc(s.corr, 1)
+    V.wait_ge(s.s2, 1)
+    V.reciprocal(T.rstd[:, 0:1], T.sroot[:, 0:1]).then_inc(s.v4, 1)
     PE.wait_ge(s.diag, 1)
-    PE.matmul(T.p_y[:, 0:128], T.s1[:], T.diag[:], True, True).then_inc(s.y, 1)
-    V.wait_ge(s.y, 1)
-    V.tensor_copy(T.ysb[:], T.p_y[:, 0:128]).then_inc(s.yc, 1)
+    PE.wait_ge(s.c3, 1)
+    PE.matmul(T.p_r[:, 0:128], T.onesT[:], T.diag[:], True, True).then_inc(s.r, 1)
+
+    V.wait_ge(s.corr, 1)
+    V.wait_ge(s.ownp, 1)
+    V.wait_ge(s.arr2, n_eng * (N - 1))
+    V.tensor_tensor(T.s1[:], T.sg[:, 0:128], T.p_corr[:, 0:128], add).then_inc(s.sum, 1)
+    V.wait_ge(s.sum, 1)
+    V.wait_ge(s.r, 1)
+    V.tensor_tensor(T.ysb[:], T.s1[:], T.p_r[:, 0:128], mult).then_inc(s.yc, 1)
     SY.wait_ge(s.yc, 1)
     SY.dma_start(T.y[:], T.ysb[:]).then_inc(s.st, 16)
     SY.wait_ge(s.st, 16)

@@ -5,11 +5,11 @@ N = 7
 PW = 20
 WIN = 24
 NP = N * PW
-NZ = NP + 4
 PER = 2 * PW + 4
 SNDW = PER * (N // 2) + WIN
 D = 128 * N
 EPS = 0.01
+KB = 16
 
 SCRATCH = {
     "xs": ("sbuf", [128, 128], "float32"),
@@ -18,7 +18,10 @@ SCRATCH = {
     "onesT": ("sbuf", [128, 128], "float32"),
     "ident": ("sbuf", [128, 128], "float32"),
     "cst": ("sbuf", [128, 8], "float32"),
-    "z": ("sbuf", [128, NZ], "float32"),
+    "z": ("sbuf", [128, NP], "float32"),
+    "c7": ("sbuf", [128, 4], "float32"),
+    "cwin": ("sbuf", [128, 4], "float32"),
+    "cwb": ("sbuf", [128, KB], "float32"),
     "z2": ("sbuf", [128, 128], "float32"),
     "tmpd": ("sbuf", [128, 128], "float32"),
     "ccol": ("sbuf", [128, 4], "float32"),
@@ -31,7 +34,7 @@ SCRATCH = {
     "sg": ("sbuf", [128, NP], "float32"),
     "mus": ("sbuf", [128, 4], "float32"),
     "qp": ("sbuf", [128, 4], "float32"),
-    "d7": ("sbuf", [128, 8], "float32"),
+    "d7": ("sbuf", [128, KB], "float32"),
     "junka": ("sbuf", [128, 8], "float32"),
     "junkb": ("sbuf", [128, 8], "float32"),
     "junk7": ("sbuf", [128, 8], "float32"),
@@ -48,10 +51,12 @@ SCRATCH = {
     "p_tr": ("psum", [128, 512], "float32"),
     "p_corr": ("psum", [128, 512], "float32"),
     "p_r": ("psum", [128, 512], "float32"),
+    "p_cw": ("psum", [128, 512], "float32"),
+    "p_tw": ("psum", [128, 512], "float32"),
 }
-SEMAPHORES = ["x", "w", "c1", "c2", "c3", "c4", "c5", "id", "mb", "z", "pt", "z2", "m2", "td", "cc", "st3", "cp1",
+SEMAPHORES = ["x", "w", "c1", "c2", "c3", "c4", "c5", "c6", "id", "mb", "z", "pt", "z2", "m2", "td", "cc", "st3", "cp1",
               "ownw", "sent1", "sent2", "arr1", "arr2", "t1", "t23", "tot", "ownp", "v2", "a1", "a3", "sq", "s2", "v4",
-              "diag", "tr", "trc", "corr", "sum", "r", "yc", "st"]
+              "diag", "tr", "trw", "trc", "cwm", "cwc", "cw1", "cw2", "pr", "sent0", "corr", "sum", "r", "yc", "st"]
 
 
 def win_start(j):
@@ -70,7 +75,6 @@ def rank_program(g, core, T, topo):
     so = PW if rank % 2 == 0 else 0
     Mc = T.land1[:, so::WIN]
     Qc = T.land1[:, so + 1::WIN]
-    Wc = T.land1[:, so + 2::WIN]
     others = [(rank + k) % N for k in range(1, N)]
     mask = topo.mask(core, T.cores[others[0]])
     for d in others:
@@ -91,21 +95,30 @@ def rank_program(g, core, T, topo):
     V.memset(T.cst[:, 0:4], 1.0).then_inc(s.c2, 1)
     V.memset(T.cst[:, 4:8], 1.0 / D).then_inc(s.c2, 1)
     V.memset(T.z[:, 128:NP], 0.0).then_inc(s.c5, 1)
-    V.memset(T.z[:, NP:NZ], 1.0 / N).then_inc(s.c5, 1)
+    V.memset(T.c7[:], 1.0 / N).then_inc(s.c5, 1)
+    V.memset(T.cwb[:, 10:12], 0.0).then_inc(s.c5, 1)
     V.memset(T.snd[:], 0.0).then_inc(s.c4, 1)
+    V.memset(T.d7[:], 0.0).then_inc(s.c6, 1)
     g.wait_ge(s.c3, 1)
     g.affine_select(T.ident[:], T.onesT[:], [[-1, 128]], AluOpType.is_equal, 0.0, 0, 1).then_inc(s.id, 1)
 
     PE.wait_ge(s.x, 16)
     PE.wait_ge(s.c1, 1)
     PE.matmul(T.p_mb[:, 0:128], T.o128[:], T.xs[:], True, True).then_inc(s.mb, 1)
+    PE.wait_ge(s.w, 16)
+    PE.wait_ge(s.c5, 3)
+    PE.matmul(T.p_cw[:, 0:4], T.ws[:], T.c7[:], True, True).then_inc(s.cwm, 1)
+    ACT.wait_ge(s.cwm, 1)
+    ACT.activation(T.cwb[:, 9:10], T.p_cw[:, 0:1], AF.Identity).then_inc(s.cwc, 1)
+    g.wait_ge(s.cwc, 1)
+    g.remote_dma_fused([RemoteDMATransfer(dst_ids=[ids[(rank + 1) % N]], dma_engine_mask=mask, remote_sem=s.cw1,
+                                          srcs=[T.cwb[:, 9:10]], dsts=[T.cwin[:, 0:1]], alu_op=0)],
+                       local_sem=s.sent0)
     V.wait_ge(s.x, 16)
     V.wait_ge(s.mb, 1)
     V.tensor_tensor(T.z[:, 0:128], T.xs[:], T.p_mb[:, 0:128], sub).then_inc(s.z, 1)
-    PE.wait_ge(s.w, 16)
-    PE.wait_ge(s.c5, 2)
     PE.wait_ge(s.z, 1)
-    PE.matmul(T.p_pt[:, 0:NZ], T.ws[:], T.z[:], True, True).then_inc(s.pt, 1)
+    PE.matmul(T.p_pt[:, 0:NP], T.ws[:], T.z[:], True, True).then_inc(s.pt, 1)
     ACT.wait_ge(s.z, 1)
     ACT.activation(T.z2[:], T.z[:, 0:128], AF.Square).then_inc(s.z2, 1)
     PE.wait_ge(s.z2, 1)
@@ -125,12 +138,11 @@ def rank_program(g, core, T, topo):
         ja = a // PW
         pa = PER * (ja // 2) + (0 if ja % 2 == 0 else WIN)
         V.tensor_copy(T.snd[:, pa:pa + (b - a)], T.p_pt[:, a:b]).then_inc(s.cp1, 1)
-    V.tensor_copy(T.snd[:, PW + 2::PER], T.p_pt[:, NP:NZ]).then_inc(s.st3, 1)
     ACT.wait_ge(s.c4, 1)
     ACT.wait_ge(s.m2, 1)
     ACT.activation(T.snd[:, PW + 1::PER], T.p_st[:, 0:4], AF.Identity, bias=EPS / N).then_inc(s.st3, 1)
 
-    g.wait_ge(s.st3, 3)
+    g.wait_ge(s.st3, 2)
     g.wait_ge(s.cp1, len(runs))
     slot = T.land1[:, rank * WIN:(rank + 1) * WIN]
 
@@ -145,9 +157,20 @@ def rank_program(g, core, T, topo):
     g.remote_dma_fused([window_to(others[i], bits[i * q4:(i + 1) * q4]) for i in range(4)], local_sem=s.sent1)
     g.remote_dma_fused([window_to(others[4 + i], bits[i * h2:(i + 1) * h2]) for i in range(2)], local_sem=s.sent1)
     in1 = 4 * q4 + 2 * h2
-    V.wait_ge(s.st3, 3)
+    V.wait_ge(s.st3, 2)
     V.wait_ge(s.cp1, len(runs))
     V.tensor_copy(slot, T.snd[:, win_start(rank):win_start(rank) + WIN]).then_inc(s.ownw, 1)
+
+    ACT.wait_ge(s.cw1, n_eng)
+    ACT.activation(T.cwb[:, 8:9], T.cwin[:, 0:1], AF.Identity).then_inc(s.pr, 1)
+    g.wait_ge(s.pr, 1)
+    g.wait_ge(s.c5, 3)
+    step2 = [((rank + 2) % N, 4), ((rank + 4) % N, 0), ((rank + 6) % N, 12)]
+    g.remote_dma_fused([RemoteDMATransfer(dst_ids=[ids[d] for d, _c in step2], dma_engine_mask=mask, remote_sem=s.cw2,
+                                          srcs=[T.cwb[:, 8:12]], dsts=[T.cwb[:, c:c + 4] for _d, c in step2], alu_op=0)],
+                       local_sem=s.sent0)
+    where = [(0, (rank - 5) % N), (1, (rank - 4) % N), (4, (rank - 3) % N), (5, (rank - 2) % N), (8, (rank - 1) % N),
+             (9, rank), (13, (rank + 1) % N)]
 
     V.wait_ge(s.ownw, 1)
     V.wait_ge(s.arr1, in1)
@@ -165,6 +188,7 @@ def rank_program(g, core, T, topo):
                        local_sem=s.sent2)
     g.wait_ge(s.sent1, in1)
     g.wait_ge(s.sent2, n_eng)
+    g.wait_ge(s.sent0, 2 * n_eng)
 
     ACT.wait_ge(s.ownw, 1)
     ACT.wait_ge(s.arr1, in1)
@@ -182,18 +206,32 @@ def rank_program(g, core, T, topo):
     ACT.activation(T.diag[:], T.ident[:], AF.Identity, scale=T.rstd[:, 0:1]).then_inc(s.diag, 1)
 
     V.wait_ge(s.tot, 1)
-    V.tensor_scalar(T.d7[:, 0:N], Mc, float(N), T.tot[:, so:so + 1], mult, sub).then_inc(s.v2, 1)
+    V.wait_ge(s.c6, 1)
+    nd = 0
+    i = 0
+    while i < len(where):
+        c, r = where[i]
+        two = i + 1 < len(where) and where[i + 1][0] == c + 1 and where[i + 1][1] == r + 1
+        k = 2 if two else 1
+        V.tensor_scalar(T.d7[:, c:c + k], T.land1[:, so + WIN * r:so + WIN * (r + k - 1) + 1:WIN], float(N),
+                        T.tot[:, so:so + 1], mult, sub).then_inc(s.v2, 1)
+        nd += 1
+        i += k
     V.tensor_copy(piece, T.tot[:, po:po + PW]).then_inc(s.ownp, 1)
-    PE.wait_ge(s.ownw, 1)
-    PE.wait_ge(s.arr1, in1)
     PE.wait_ge(s.id, 1)
-    PE.matmul(T.p_tr[0:N, 128:256], Wc, T.ident[:], True, True).then_inc(s.tr, 1)
-    PE.wait_ge(s.v2, 1)
-    PE.matmul(T.p_tr[0:N, 0:128], T.d7[:, 0:N], T.ident[:], True, True).then_inc(s.tr, 1)
-    V.wait_ge(s.tr, 2)
-    V.tensor_copy(T.tr[0:N, 0:256], T.p_tr[0:N, 0:256]).then_inc(s.trc, 1)
-    PE.wait_ge(s.trc, 1)
-    PE.matmul(T.p_corr[:, 0:128], T.tr[0:N, 128:256], T.tr[0:N, 0:128], True, True).then_inc(s.corr, 1)
+    PE.wait_ge(s.cwc, 1)
+    PE.wait_ge(s.pr, 1)
+    PE.wait_ge(s.cw2, 3 * n_eng)
+    PE.matmul(T.p_tw[0:KB, 0:128], T.cwb[:], T.ident[:], True, True).then_inc(s.trw, 1)
+    PE.wait_ge(s.c6, 1)
+    PE.wait_ge(s.v2, nd)
+    PE.matmul(T.p_tr[0:KB, 0:128], T.d7[:], T.ident[:], True, True).then_inc(s.tr, 1)
+    V.wait_ge(s.trw, 1)
+    V.tensor_copy(T.tr[0:KB, 128:256], T.p_tw[0:KB, 0:128]).then_inc(s.trc, 1)
+    V.wait_ge(s.tr, 1)
+    V.tensor_copy(T.tr[0:KB, 0:128], T.p_tr[0:KB, 0:128]).then_inc(s.trc, 1)
+    PE.wait_ge(s.trc, 2)
+    PE.matmul(T.p_corr[:, 0:128], T.tr[0:KB, 128:256], T.tr[0:KB, 0:128], True, True).then_inc(s.corr, 1)
     V.wait_ge(s.s2, 1)
     V.reciprocal(T.rstd[:, 0:1], T.sroot[:, 0:1]).then_inc(s.v4, 1)
     PE.wait_ge(s.diag, 1)

from concourse.bass import DstId, RemoteDMATransfer
from concourse.mybir import AluOpType, AxisListType, ActivationFunctionType

N = 7
PW = 20
WIN = 24
NP = N * PW
PER = 2 * PW + 4
SNDW = PER * (N // 2) + WIN
D = 128 * N
EPS = 0.01
KB = 16

SCRATCH = {
    "xs": ("sbuf", [128, 128], "float32"),
    "ws": ("sbuf", [128, 128], "float32"),
    "o128": ("sbuf", [128, 128], "float32"),
    "onesT": ("sbuf", [128, 128], "float32"),
    "ident": ("sbuf", [128, 128], "float32"),
    "cst": ("sbuf", [128, 8], "float32"),
    "z": ("sbuf", [128, NP], "float32"),
    "c7": ("sbuf", [128, 4], "float32"),
    "cwin": ("sbuf", [128, 4], "float32"),
    "cwb": ("sbuf", [128, KB], "float32"),
    "z2": ("sbuf", [128, 128], "float32"),
    "tmpd": ("sbuf", [128, 128], "float32"),
    "ccol": ("sbuf", [128, 4], "float32"),
    "snd": ("sbuf", [128, SNDW], "float32"),
    "land1": ("sbuf", [128, N * WIN], "float32"),
    "t1": ("sbuf", [128, 3 * WIN], "float32"),
    "t2": ("sbuf", [128, WIN], "float32"),
    "t3": ("sbuf", [128, WIN], "float32"),
    "tot": ("sbuf", [128, WIN], "float32"),
    "sg": ("sbuf", [128, NP], "float32"),
    "mus": ("sbuf", [128, 4], "float32"),
    "qp": ("sbuf", [128, 4], "float32"),
    "d7": ("sbuf", [128, KB], "float32"),
    "junka": ("sbuf", [128, 8], "float32"),
    "junkb": ("sbuf", [128, 8], "float32"),
    "junk7": ("sbuf", [128, 8], "float32"),
    "sd49": ("sbuf", [128, 4], "float32"),
    "sroot": ("sbuf", [128, 4], "float32"),
    "rstd": ("sbuf", [128, 4], "float32"),
    "diag": ("sbuf", [128, 128], "float32"),
    "tr": ("sbuf", [128, 256], "float32"),
    "s1": ("sbuf", [128, 128], "float32"),
    "ysb": ("sbuf", [128, 128], "float32"),
    "p_mb": ("psum", [128, 512], "float32"),
    "p_pt": ("psum", [128, 512], "float32"),
    "p_st": ("psum", [128, 512], "float32"),
    "p_tr": ("psum", [128, 512], "float32"),
    "p_corr": ("psum", [128, 512], "float32"),
    "p_r": ("psum", [128, 512], "float32"),
    "p_cw": ("psum", [128, 512], "float32"),
    "p_tw": ("psum", [128, 512], "float32"),
}
SEMAPHORES = ["x", "w", "c1", "c2", "c3", "c4", "c5", "c6", "id", "mb", "z", "pt", "z2", "m2", "td", "cc", "st3", "cp1",
              "ownw", "sent1", "sent2", "arr1", "arr2", "t1", "t23", "tot", "ownp", "v2", "a1", "a3", "sq", "s2", "v4",
              "diag", "tr", "trw", "trc", "cwm", "cwc", "cw1", "cw2", "pr", "sent0", "corr", "sum", "r", "yc", "st"]


def win_start(j):
    return PER * (j // 2) + (0 if j % 2 == 0 else PW)


def rank_program(g, core, T, topo):
    rank = T.rank_of(core)
    if rank is None:
        return
    s = T.sem
    V, PE, ACT, SY = g.vector, g.tensor, g.scalar, g.sync
    add, mult, sub = AluOpType.add, AluOpType.mult, AluOpType.subtract
    AF = ActivationFunctionType
    po = 0 if rank % 2 == 0 else 4
    so = PW if rank % 2 == 0 else 0
    Mc = T.land1[:, so::WIN]
    Qc = T.land1[:, so + 1::WIN]
    others = [(rank + k) % N for k in range(1, N)]
    mask = topo.mask(core, T.cores[others[0]])
    for d in others:
        if not topo.may_write(core, T.cores[d]):
            raise ValueError("rank core cannot reach a rank")
        mask &= topo.mask(core, T.cores[d])
    bits = [b for b in range(16) if (mask >> b) & 1]
    n_eng = len(bits)
    ids = {}
    for d in others:
        rid, pid, _se = topo.addr(T.cores[d])
        ids[d] = DstId(rid=rid, pnc=pid)

    SY.dma_start(T.xs[:], T.x[:]).then_inc(s.x, 16)
    ACT.dma_start(T.ws[:], T.w[:]).then_inc(s.w, 16)
    V.memset(T.o128[:], 1.0 / 128).then_inc(s.c1, 1)
    V.memset(T.onesT[:], 1.0).then_inc(s.c3, 1)
    V.memset(T.cst[:, 0:4], 1.0).then_inc(s.c2, 1)
    V.memset(T.cst[:, 4:8], 1.0 / D).then_inc(s.c2, 1)
    V.memset(T.z[:, 128:NP], 0.0).then_inc(s.c5, 1)
    V.memset(T.c7[:], 1.0 / N).then_inc(s.c5, 1)
    V.memset(T.cwb[:, 10:12], 0.0).then_inc(s.c5, 1)
    V.memset(T.snd[:], 0.0).then_inc(s.c4, 1)
    V.memset(T.d7[:], 0.0).then_inc(s.c6, 1)
    g.wait_ge(s.c3, 1)
    g.affine_select(T.ident[:], T.onesT[:], [[-1, 128]], AluOpType.is_equal, 0.0, 0, 1).then_inc(s.id, 1)

    PE.wait_ge(s.x, 16)
    PE.wait_ge(s.c1, 1)
    PE.matmul(T.p_mb[:, 0:128], T.o128[:], T.xs[:], True, True).then_inc(s.mb, 1)
    PE.wait_ge(s.w, 16)
    PE.wait_ge(s.c5, 3)
    PE.matmul(T.p_cw[:, 0:4], T.ws[:], T.c7[:], True, True).then_inc(s.cwm, 1)
    ACT.wait_ge(s.cwm, 1)
    ACT.activation(T.cwb[:, 9:10], T.p_cw[:, 0:1], AF.Identity).then_inc(s.cwc, 1)
    g.wait_ge(s.cwc, 1)
    g.remote_dma_fused([RemoteDMATransfer(dst_ids=[ids[(rank + 1) % N]], dma_engine_mask=mask, remote_sem=s.cw1,
                                          srcs=[T.cwb[:, 9:10]], dsts=[T.cwin[:, 0:1]], alu_op=0)],
                       local_sem=s.sent0)
    V.wait_ge(s.x, 16)
    V.wait_ge(s.mb, 1)
    V.tensor_tensor(T.z[:, 0:128], T.xs[:], T.p_mb[:, 0:128], sub).then_inc(s.z, 1)
    PE.wait_ge(s.z, 1)
    PE.matmul(T.p_pt[:, 0:NP], T.ws[:], T.z[:], True, True).then_inc(s.pt, 1)
    ACT.wait_ge(s.z, 1)
    ACT.activation(T.z2[:], T.z[:, 0:128], AF.Square).then_inc(s.z2, 1)
    PE.wait_ge(s.z2, 1)
    PE.wait_ge(s.c2, 2)
    PE.matmul(T.p_st[:, 0:4], T.z2[:], T.cst[:, 4:8], True, True).then_inc(s.m2, 1)
    V.wait_ge(s.id, 1)
    V.tensor_tensor(T.tmpd[:], T.ident[:], T.p_mb[:, 0:128], mult).then_inc(s.td, 1)
    V.wait_ge(s.td, 1)
    V.tensor_reduce(T.ccol[:, 0:1], T.tmpd[:], AxisListType.X, add).then_inc(s.cc, 1)
    V.wait_ge(s.cc, 1)
    V.wait_ge(s.c2, 2)
    V.wait_ge(s.c4, 1)
    V.tensor_scalar(T.snd[:, PW::PER], T.cst[:, 0:4], T.ccol[:, 0:1], None, mult).then_inc(s.st3, 1)
    V.wait_ge(s.pt, 1)
    runs = [(0, PW)] + [(PW + 2 * PW * i, 3 * PW + 2 * PW * i) for i in range(N // 2)]
    for a, b in runs:
        ja = a // PW
        pa = PER * (ja // 2) + (0 if ja % 2 == 0 else WIN)
        V.tensor_copy(T.snd[:, pa:pa + (b - a)], T.p_pt[:, a:b]).then_inc(s.cp1, 1)
    ACT.wait_ge(s.c4, 1)
    ACT.wait_ge(s.m2, 1)
    ACT.activation(T.snd[:, PW + 1::PER], T.p_st[:, 0:4], AF.Identity, bias=EPS / N).then_inc(s.st3, 1)

    g.wait_ge(s.st3, 2)
    g.wait_ge(s.cp1, len(runs))
    slot = T.land1[:, rank * WIN:(rank + 1) * WIN]

    def window_to(d, engines):
        m = 0
        for b in engines:
            m |= 1 << b
        return RemoteDMATransfer(dst_ids=[ids[d]], dma_engine_mask=m, remote_sem=s.arr1,
                                 srcs=[T.snd[:, win_start(d):win_start(d) + WIN]], dsts=[slot], alu_op=0)

    q4, h2 = n_eng // 4, n_eng // 2
    g.remote_dma_fused([window_to(others[i], bits[i * q4:(i + 1) * q4]) for i in range(4)], local_sem=s.sent1)
    g.remote_dma_fused([window_to(others[4 + i], bits[i * h2:(i + 1) * h2]) for i in range(2)], local_sem=s.sent1)
    in1 = 4 * q4 + 2 * h2
    V.wait_ge(s.st3, 2)
    V.wait_ge(s.cp1, len(runs))
    V.tensor_copy(slot, T.snd[:, win_start(rank):win_start(rank) + WIN]).then_inc(s.ownw, 1)

    ACT.wait_ge(s.cw1, n_eng)
    ACT.activation(T.cwb[:, 8:9], T.cwin[:, 0:1], AF.Identity).then_inc(s.pr, 1)
    g.wait_ge(s.pr, 1)
    g.wait_ge(s.c5, 3)
    step2 = [((rank + 2) % N, 4), ((rank + 4) % N, 0), ((rank + 6) % N, 12)]
    g.remote_dma_fused([RemoteDMATransfer(dst_ids=[ids[d] for d, _c in step2], dma_engine_mask=mask, remote_sem=s.cw2,
                                          srcs=[T.cwb[:, 8:12]], dsts=[T.cwb[:, c:c + 4] for _d, c in step2], alu_op=0)],
                       local_sem=s.sent0)
    where = [(0, (rank - 5) % N), (1, (rank - 4) % N), (4, (rank - 3) % N), (5, (rank - 2) % N), (8, (rank - 1) % N),
             (9, rank), (13, (rank + 1) % N)]

    V.wait_ge(s.ownw, 1)
    V.wait_ge(s.arr1, in1)
    V.tensor_tensor(T.t1[:], T.land1[:, 0:3 * WIN], T.land1[:, 3 * WIN:6 * WIN], add).then_inc(s.t1, 1)
    V.wait_ge(s.t1, 1)
    V.tensor_tensor(T.t2[:], T.t1[:, 0:WIN], T.t1[:, WIN:2 * WIN], add).then_inc(s.t23, 1)
    V.tensor_tensor(T.t3[:], T.t1[:, 2 * WIN:3 * WIN], T.land1[:, 6 * WIN:7 * WIN], add).then_inc(s.t23, 1)
    V.wait_ge(s.t23, 2)
    V.tensor_tensor(T.tot[:], T.t2[:], T.t3[:], add).then_inc(s.tot, 1)

    g.wait_ge(s.tot, 1)
    piece = T.sg[:, rank * PW:(rank + 1) * PW]
    g.remote_dma_fused([RemoteDMATransfer(dst_ids=[ids[d] for d in others], dma_engine_mask=mask, remote_sem=s.arr2,
                                          srcs=[T.tot[:, po:po + PW]], dsts=[piece for _d in others], alu_op=0)],
                       local_sem=s.sent2)
    g.wait_ge(s.sent1, in1)
    g.wait_ge(s.sent2, n_eng)
    g.wait_ge(s.sent0, 2 * n_eng)

    ACT.wait_ge(s.ownw, 1)
    ACT.wait_ge(s.arr1, in1)
    ACT.activation(T.junka[:, 0:N], Mc, AF.Identity, accum_out=T.mus[:, 0:1]).then_inc(s.a1, 1)
    ACT.activation(T.junkb[:, 0:N], Qc, AF.Identity, accum_out=T.qp[:, 0:1]).then_inc(s.a3, 1)
    ACT.wait_ge(s.a1, 1)
    ACT.activation(T.junk7[:, 0:N], Mc, AF.Square, bias=T.mus[:, 0:1], scale=-float(N),
                   accum_out=T.sd49[:, 0:1]).then_inc(s.sq, 1)
    ACT.wait_ge(s.sq, 1)
    ACT.wait_ge(s.a3, 1)
    ACT.activation(T.sroot[:, 0:1], T.sd49[:, 0:1], AF.Sqrt, bias=T.qp[:, 0:1],
                   scale=128.0 / (N * N * D)).then_inc(s.s2, 1)
    ACT.wait_ge(s.v4, 1)
    ACT.wait_ge(s.id, 1)
    ACT.activation(T.diag[:], T.ident[:], AF.Identity, scale=T.rstd[:, 0:1]).then_inc(s.diag, 1)

    V.wait_ge(s.tot, 1)
    V.wait_ge(s.c6, 1)
    nd = 0
    i = 0
    while i < len(where):
        c, r = where[i]
        two = i + 1 < len(where) and where[i + 1][0] == c + 1 and where[i + 1][1] == r + 1
        k = 2 if two else 1
        V.tensor_scalar(T.d7[:, c:c + k], T.land1[:, so + WIN * r:so + WIN * (r + k - 1) + 1:WIN], float(N),
                        T.tot[:, so:so + 1], mult, sub).then_inc(s.v2, 1)
        nd += 1
        i += k
    V.tensor_copy(piece, T.tot[:, po:po + PW]).then_inc(s.ownp, 1)
    PE.wait_ge(s.id, 1)
    PE.wait_ge(s.cwc, 1)
    PE.wait_ge(s.pr, 1)
    PE.wait_ge(s.cw2, 3 * n_eng)
    PE.matmul(T.p_tw[0:KB, 0:128], T.cwb[:], T.ident[:], True, True).then_inc(s.trw, 1)
    PE.wait_ge(s.c6, 1)
    PE.wait_ge(s.v2, nd)
    PE.matmul(T.p_tr[0:KB, 0:128], T.d7[:], T.ident[:], True, True).then_inc(s.tr, 1)
    V.wait_ge(s.trw, 1)
    V.tensor_copy(T.tr[0:KB, 128:256], T.p_tw[0:KB, 0:128]).then_inc(s.trc, 1)
    V.wait_ge(s.tr, 1)
    V.tensor_copy(T.tr[0:KB, 0:128], T.p_tr[0:KB, 0:128]).then_inc(s.trc, 1)
    PE.wait_ge(s.trc, 2)
    PE.matmul(T.p_corr[:, 0:128], T.tr[0:KB, 128:256], T.tr[0:KB, 0:128], True, True).then_inc(s.corr, 1)
    V.wait_ge(s.s2, 1)
    V.reciprocal(T.rstd[:, 0:1], T.sroot[:, 0:1]).then_inc(s.v4, 1)
    PE.wait_ge(s.diag, 1)
    PE.wait_ge(s.c3, 1)
    PE.matmul(T.p_r[:, 0:128], T.onesT[:], T.diag[:], True, True).then_inc(s.r, 1)

    V.wait_ge(s.corr, 1)
    V.wait_ge(s.ownp, 1)
    V.wait_ge(s.arr2, n_eng * (N - 1))
    V.tensor_tensor(T.s1[:], T.sg[:, 0:128], T.p_corr[:, 0:128], add).then_inc(s.sum, 1)
    V.wait_ge(s.sum, 1)
    V.wait_ge(s.r, 1)
    V.tensor_tensor(T.ysb[:], T.s1[:], T.p_r[:, 0:128], mult).then_inc(s.yc, 1)
    SY.wait_ge(s.yc, 1)
    SY.dma_start(T.y[:], T.ysb[:]).then_inc(s.st, 16)
    SY.wait_ge(s.st, 16)
